import numpy as np
import ml_dtypes


def mxq(x, axis, fmt="e4m3"):
    dtype, down = {"e4m3": (ml_dtypes.float8_e4m3fn, 7), "e5m2": (ml_dtypes.float8_e5m2, 14)}[fmt]
    v = np.moveaxis(np.asarray(x, np.float32).astype(ml_dtypes.bfloat16).astype(np.float64), axis, -1)
    blocks = v.reshape(v.shape[:-1] + (-1, 32))
    amax = np.abs(blocks).max(-1, keepdims=True)
    byte = np.maximum(np.where(amax > 0, np.frexp(amax)[1] - 1 + 127, 0) - down, 1)
    scale = np.exp2(byte - 127.0)
    codes = (blocks / scale).astype(np.float32).astype(dtype).astype(np.float64)
    return np.moveaxis((codes * scale).reshape(v.shape), -1, axis)


WIDE = False


def mx_kscale(k):
    if not WIDE:
        return np.ones(k)
    levels = np.array([10, -10, 5, -5, 0])
    if k % 512:
        return np.exp2(np.random.permutation(np.resize(levels, k // 32))).repeat(32)
    a = np.empty((k // 512, 16))
    for p in range(k // 512):
        a[p, :8] = np.random.permutation(np.resize(levels, 8))
        for g in range(8):
            far = levels[np.abs(levels - a[p, g]) >= 10]
            a[p, g + 8] = far[np.random.randint(len(far))]
    return np.exp2(a.ravel()).repeat(32)


def f64(x):
    return np.asarray(x).astype(np.float64)


def striped(idx):
    return np.tile(idx.reshape(-1, 16).T, (8, 1)).astype(np.uint16)


def unstriped(offs):
    return offs[:16].T.reshape(-1).astype(np.int64)


def gelu(v):
    return 0.5 * v * (1.0 + np.tanh(np.sqrt(2.0 / np.pi) * (v + 0.044715 * v**3)))


K, T, E, C, H, N = 1536, 1536, 4, 128, 512, 128


def by_expert(wq, xq):
    return np.concatenate([wq[e].T @ xq[:, e * C:(e + 1) * C] for e in range(E)], axis=1)


def setup_inputs():
    n = np.random.standard_normal
    s = mx_kscale(K)[:, None]
    u = mx_kscale(H)
    return {
        "xT": (n((K, T)) * s).astype(np.float32),
        "w1": (n((E, K, H)) / np.sqrt(K) / s[None] * u[None, None, :]).astype(np.float32),
        "w2": (n((E, H, N)) / np.sqrt(H) / u[None, :, None]).astype(np.float32),
        "gate": np.tile(np.random.uniform(0.2, 1.0, E * C), (N, 1)).astype(np.float32),
        "offs": striped(np.random.permutation(T)[:E * C]),
    }


def reference(xT, w1, w2, gate, offs):
    idx = unstriped(offs)
    xq = mxq(f64(xT)[:, idx], 0, "e4m3")
    h = gelu(by_expert(mxq(f64(w1), 1, "e4m3"), xq))
    y = by_expert(mxq(f64(w2), 1, "e4m3"), mxq(h, 0, "e4m3"))
    out = np.zeros((N, T))
    out[:, idx] = f64(gate) * y
    return out

@@ -1,0 +1,216 @@
+from contextlib import ExitStack
+
+import concourse.mybir as mybir
+
+K, T, E, C, H, N = 1536, 1536, 4, 128, 512, 128
+SLOTS = E * C
+P = 128
+PACK = 4
+K_PASS = P * PACK
+PASSES = K // K_PASS
+FLOPS = 2 * SLOTS * (K * H + H * N)
+
+F32 = mybir.dt.float32
+BF16 = mybir.dt.bfloat16
+U32 = mybir.dt.uint32
+U16 = mybir.dt.uint16
+U8 = mybir.dt.uint8
+FP8X4 = mybir.dt.float8_e4m3fn_x4
+GELU = mybir.ActivationFunctionType.Gelu_apprx_tanh
+MULT = mybir.AluOpType.mult
+
+SCALAR_M = 72
+LAST_SCALAR_M = 44
+
+
+def tile_routed_moe_kernel(tc, xT, w1, w2, gate, offs, out):
+    nc = tc.nc
+    with ExitStack() as ctx:
+        keep = ctx.enter_context(tc.tile_pool(name="keep", bufs=1))
+        raws = ctx.enter_context(tc.tile_pool(name="raws", bufs=5))
+        work = ctx.enter_context(tc.tile_pool(name="work", bufs=2))
+        psum = ctx.enter_context(tc.psum_pool(name="psum", bufs=2))
+
+        offsets = keep.tile([P, SLOTS // 16], U16, name="offsets")
+        nc.sync.dma_start(offsets[:], offs)
+
+        x_raw = []
+        for s in range(PASSES):
+            raw = raws.tile([P, PACK * T], F32, name=f"x_raw{s}", tag="raw")
+            for j in range(PACK):
+                nc.sync.dma_start(
+                    out=raw[:, j * T:(j + 1) * T],
+                    in_=xT[s * K_PASS:(s + 1) * K_PASS, :].rearrange("(p j) n -> p j n", j=PACK)[:, j, :],
+                )
+            x_raw.append(raw)
+        w2_raw = keep.tile([P, E, PACK * N], F32, name="w2_raw")
+        gates = keep.tile([P, SLOTS], F32, name="gates")
+
+        def load_pair(first):
+            pair, cols = slice(first, first + 2), slice(first * C, (first + 2) * C)
+            nc.sync.dma_start(out=w2_raw[:, pair, :], in_=w2[pair].rearrange("e (p j) n -> p e (j n)", j=PACK))
+            nc.sync.dma_start(out=gates[:, cols], in_=gate[:, cols])
+
+        load_pair(0)
+        w1_raw = []
+        for e in range(E):
+            raw = raws.tile([P, PASSES * PACK * H], F32, name=f"w1_raw{e}", tag="raw")
+            src = w1[e].rearrange("(s p j) c -> p s (j c)", p=P, j=PACK)
+            dst = raw[:].rearrange("p (s f) -> p s f", s=PASSES)
+            for s in range(PASSES):
+                nc.sync.dma_start(out=dst[:, s, :], in_=src[:, s, :])
+            w1_raw.append(raw)
+        load_pair(2)
+
+        window = keep.tile([P, T], F32, name="window")
+        nc.gpsimd.memset(window[:], 0.0)
+        warm = keep.tile([P, 1], F32, name="warm")
+        nc.gpsimd.memset(warm[:], 0.0)
+        nc.scalar.activation(warm[:], warm[:], GELU)
+
+        x_codes = keep.tile([P, PASSES, SLOTS], U32, name="x_codes", align_bytes=64)
+        x_scales = keep.tile([P, PASSES, SLOTS], U8, name="x_scales", align_bytes=64)
+        picked, x_grouped = {}, {}
+
+        def gather(s):
+            picked[s] = work.tile([P, PACK, SLOTS], F32, name=f"picked{s}", tag="picked")
+            for j in range(PACK):
+                nc.vector.tensor_copy(picked[s][:, j, :], x_raw[s][:, j * T:(j + 1) * T].indirect(offsets[:]))
+
+        def group_tokens(s):
+            x_grouped[s] = work.tile([P, SLOTS * PACK], BF16, name=f"x_grouped{s}", tag="x_grouped", align_bytes=64)
+            nc.scalar.copy(
+                out=x_grouped[s][:].rearrange("p (c i j) -> p c j i", i=4, j=PACK),
+                in_=picked[s][:].rearrange("p j (c i) -> p c j i", i=4),
+            )
+
+        def quantize_tokens(s):
+            nc.vector.quantize_mx(out=x_codes[:, s, :].bitcast(FP8X4), scales=x_scales[:, s, :], in_=x_grouped[s][:])
+
+        w2_codes = keep.tile([P, E, N], U32, name="w2_codes", align_bytes=64)
+        w2_scales = keep.tile([P, E, N], U8, name="w2_scales", align_bytes=64)
+        w2_grouped = keep.tile([P, E, N * PACK], BF16, name="w2_grouped", align_bytes=64)
+
+        def group_w2(first):
+            nc.scalar.copy(
+                out=w2_grouped[:, first:first + 2, :].rearrange("p e (c j) -> p e c j", j=PACK),
+                in_=w2_raw[:, first:first + 2, :].rearrange("p e (j c) -> p e c j", j=PACK),
+            )
+
+        def quantize_w2(first):
+            nc.vector.quantize_mx(
+                out=w2_codes[:, first:first + 2, :].rearrange("p e n -> p (e n)").bitcast(FP8X4),
+                scales=w2_scales[:, first:first + 2, :].rearrange("p e n -> p (e n)"),
+                in_=w2_grouped[:, first:first + 2, :].rearrange("p e f -> p (e f)"),
+            )
+
+        y_all = keep.tile([P, SLOTS], F32, name="y_all")
+        w1_codes, w1_scales, w1_grouped, acc, hidden, ys = {}, {}, {}, {}, {}, {}
+
+        def group_w1(e, s):
+            grouped = work.tile([P, H * PACK], BF16, name=f"w1_grouped{e}{s}", tag="w1_grouped", align_bytes=64, bufs=4)
+            dst = grouped[:].rearrange("p (t m j) -> p m t j", t=4, j=PACK)
+            src = w1_raw[e][:, s * PACK * H:(s + 1) * PACK * H].rearrange("p (j m t) -> p m t j", j=PACK, t=4)
+            cut = LAST_SCALAR_M if (e, s) == (E - 1, PASSES - 1) else SCALAR_M
+            nc.scalar.copy(out=dst[:, 0:cut], in_=src[:, 0:cut])
+            nc.vector.tensor_copy(out=dst[:, cut:P], in_=src[:, cut:P])
+            w1_grouped[e, s] = grouped
+
+        def quantize_w1(e, s):
+            if s == 0:
+                w1_codes[e] = work.tile([P, PASSES, H], U32, name=f"w1_codes{e}", tag="w1_codes", align_bytes=64)
+                w1_scales[e] = work.tile([P, PASSES, H], U8, name=f"w1_scales{e}", tag="w1_scales", align_bytes=64)
+            nc.vector.quantize_mx(
+                out=w1_codes[e][:, s, :].bitcast(FP8X4), scales=w1_scales[e][:, s, :], in_=w1_grouped[e, s][:]
+            )
+
+        def pass_w1(e, s, t):
+            cols, slots = slice(t * P, (t + 1) * P), slice(e * C, (e + 1) * C)
+            nc.tensor.matmul_mx(
+                out=acc[e, t // 2][:, t % 2, :],
+                lhsT=w1_codes[e][:, s, cols].bitcast(FP8X4),
+                lhsT_scale=w1_scales[e][:, s, cols],
+                rhs=x_codes[:, s, slots].bitcast(FP8X4),
+                rhs_scale=x_scales[:, s, slots],
+                start=(s == 0),
+                stop=(s == PASSES - 1),
+            )
+
+        def multiply_w1(e, s):
+            for q in range(2):
+                if s == 0:
+                    acc[e, q] = psum.tile([P, 2, C], F32, name=f"acc{e}{q}", tag=f"acc{q}")
+                pass_w1(e, s, 2 * q)
+                if s == PASSES - 1:
+                    for r in range(PASSES):
+                        pass_w1(e, r, 2 * q + 1)
+
+        h_all = keep.tile([P, E, C * 4], BF16, name="h_all", align_bytes=64)
+
+        def apply_gelu(e):
+            for q in range(2):
+                nc.scalar.activation(
+                    h_all[:, e, :].rearrange("p (n q t) -> p q n t", q=2, t=2)[:, q],
+                    acc[e, q][:].rearrange("p t n -> p n t"),
+                    GELU,
+                )
+
+        def multiply_w2(first, last):
+            count = last - first
+            h_codes = keep.tile([P, count, C], U32, name=f"h_codes{first}", align_bytes=64)
+            h_scales = keep.tile([P, count, C], U8, name=f"h_scales{first}", align_bytes=64)
+            nc.vector.quantize_mx(
+                out=h_codes[:].rearrange("p e c -> p (e c)").bitcast(FP8X4),
+                scales=h_scales[:].rearrange("p e c -> p (e c)"),
+                in_=h_all[:, first:last, :].rearrange("p e f -> p (e f)"),
+            )
+            ys[first] = psum.tile([P, count, C], F32, name=f"y{first}", tag="y")
+            for e in range(first, last):
+                nc.tensor.matmul_mx(
+                    out=ys[first][:, e - first, :],
+                    lhsT=w2_codes[:, e, :].bitcast(FP8X4),
+                    lhsT_scale=w2_scales[:, e, :],
+                    rhs=h_codes[:, e - first, :].bitcast(FP8X4),
+                    rhs_scale=h_scales[:, e - first, :],
+                    start=True,
+                    stop=True,
+                )
+
+        def take_out(first, last):
+            nc.scalar.copy(y_all[:, first * C:last * C], ys[first][:].rearrange("p e c -> p (e c)"))
+
+        def put_back(a, b):
+            nc.vector.tensor_tensor(
+                window[:].indirect(offsets[:, a // 16:b // 16]), y_all[:, a:b], gates[:, a:b], MULT
+            )
+
+        gather(0)
+        group_tokens(0)
+        gather(1)
+        quantize_tokens(0)
+        group_tokens(1)
+        gather(2)
+        quantize_tokens(1)
+        group_tokens(2)
+        group_w2(0)
+        quantize_tokens(2)
+        quantize_w2(0)
+        for e in range(E):
+            for s in range(PASSES):
+                group_w1(e, s)
+                quantize_w1(e, s)
+                multiply_w1(e, s)
+                if s == 0 and e > 0:
+                    apply_gelu(e - 1)
+                if s == 1 and e == 2:
+                    multiply_w2(0, 2)
+                    take_out(0, 2)
+                if s == 2 and e == 2:
+                    put_back(0, 256)
+        group_w2(2)
+        quantize_w2(2)
+        apply_gelu(E - 1)
+        multiply_w2(2, 4)
+        take_out(2, 4)
+        put_back(256, 512)
+        nc.sync.dma_start(out=out, in_=window[:])

@@ -19,48 +19,61 @@ FP8X4 = mybir.dt.float8_e4m3fn_x4
 GELU = mybir.ActivationFunctionType.Gelu_apprx_tanh
 MULT = mybir.AluOpType.mult
 
-SCALAR_M = 72
-LAST_SCALAR_M = 44
-
 
 def tile_routed_moe_kernel(tc, xT, w1, w2, gate, offs, out):
     nc = tc.nc
     with ExitStack() as ctx:
         keep = ctx.enter_context(tc.tile_pool(name="keep", bufs=1))
-        raws = ctx.enter_context(tc.tile_pool(name="raws", bufs=5))
+        raws = ctx.enter_context(tc.tile_pool(name="raws", bufs=2))
         work = ctx.enter_context(tc.tile_pool(name="work", bufs=2))
-        psum = ctx.enter_context(tc.psum_pool(name="psum", bufs=2))
+        psum = ctx.enter_context(tc.psum_pool(name="psum", bufs=1))
 
         offsets = keep.tile([P, SLOTS // 16], U16, name="offsets")
         nc.sync.dma_start(offsets[:], offs)
 
-        x_raw = []
-        for s in range(PASSES):
-            raw = raws.tile([P, PACK * T], F32, name=f"x_raw{s}", tag="raw")
-            for j in range(PACK):
-                nc.sync.dma_start(
-                    out=raw[:, j * T:(j + 1) * T],
-                    in_=xT[s * K_PASS:(s + 1) * K_PASS, :].rearrange("(p j) n -> p j n", j=PACK)[:, j, :],
-                )
-            x_raw.append(raw)
+        x_raw, w1_raw = {}, {}
         w2_raw = keep.tile([P, E, PACK * N], F32, name="w2_raw")
         gates = keep.tile([P, SLOTS], F32, name="gates")
+        w1_passes = w1.rearrange("e (s p j) c -> p (e s) (j c)", p=P, j=PACK)
 
-        def load_pair(first):
-            pair, cols = slice(first, first + 2), slice(first * C, (first + 2) * C)
-            nc.sync.dma_start(out=w2_raw[:, pair, :], in_=w2[pair].rearrange("e (p j) n -> p e (j n)", j=PACK))
-            nc.sync.dma_start(out=gates[:, cols], in_=gate[:, cols])
+        def load_x(s, width):
+            x_raw[s] = raws.tile([P, PACK * T], F32, name=f"x_raw{s}", tag="x_raw", bufs=3)
+            rows = xT[s * K_PASS:(s + 1) * K_PASS, :].rearrange("(p j) n -> p (j n)", j=PACK)
+            for j in range(0, PACK, width):
+                cols = slice(j * T, (j + width) * T)
+                nc.sync.dma_start(out=x_raw[s][:, cols], in_=rows[:, cols])
 
-        load_pair(0)
-        w1_raw = []
-        for e in range(E):
-            raw = raws.tile([P, PASSES * PACK * H], F32, name=f"w1_raw{e}", tag="raw")
-            src = w1[e].rearrange("(s p j) c -> p s (j c)", p=P, j=PACK)
-            dst = raw[:].rearrange("p (s f) -> p s f", s=PASSES)
-            for s in range(PASSES):
-                nc.sync.dma_start(out=dst[:, s, :], in_=src[:, s, :])
-            w1_raw.append(raw)
-        load_pair(2)
+        def load_w2(first, last):
+            nc.sync.dma_start(out=w2_raw[:, first:last, :], in_=w2[first:last].rearrange("e (p j) n -> p e (j n)", j=PACK))
+
+        def load_gate(a, b):
+            nc.sync.dma_start(out=gates[:, a:b], in_=gate[:, a:b])
+
+        def load_w1(ks, bufs):
+            raw = raws.tile([P, len(ks), PACK * H], F32, name=f"w1_raw{ks[0]}", tag=f"w1_raw{len(ks)}", bufs=bufs)
+            nc.sync.dma_start(out=raw[:], in_=w1_passes[:, ks[0]:ks[-1] + 1, :])
+            for i, k in enumerate(ks):
+                w1_raw[k] = raw[:, i, :]
+
+        load_x(0, 1)
+        load_x(1, 1)
+        load_x(2, 1)
+        load_w2(0, 2)
+        load_gate(0, 256)
+        load_w1((0,), 8)
+        load_w1((1,), 8)
+        load_w1((2,), 8)
+        load_w1((3,), 8)
+        load_w1((4,), 8)
+        load_w1((5,), 8)
+        load_w1((6,), 8)
+        load_w1((7,), 8)
+        load_w1((8,), 8)
+        load_w1((9,), 8)
+        load_w1((10,), 8)
+        load_w1((11,), 8)
+        load_w2(2, 4)
+        load_gate(256, 512)
 
         window = keep.tile([P, T], F32, name="window")
         nc.gpsimd.memset(window[:], 0.0)
@@ -91,43 +104,54 @@ def tile_routed_moe_kernel(tc, xT, w1, w2, gate, offs, out):
         w2_scales = keep.tile([P, E, N], U8, name="w2_scales", align_bytes=64)
         w2_grouped = keep.tile([P, E, N * PACK], BF16, name="w2_grouped", align_bytes=64)
 
-        def group_w2(first):
+        def group_w2(first, last):
             nc.scalar.copy(
-                out=w2_grouped[:, first:first + 2, :].rearrange("p e (c j) -> p e c j", j=PACK),
-                in_=w2_raw[:, first:first + 2, :].rearrange("p e (j c) -> p e c j", j=PACK),
+                out=w2_grouped[:, first:last, :].rearrange("p e (c i j) -> p e c j i", i=4, j=PACK),
+                in_=w2_raw[:, first:last, :].rearrange("p e (j c i) -> p e c j i", i=4, j=PACK),
             )
 
-        def quantize_w2(first):
+        def quantize_w2(first, last):
             nc.vector.quantize_mx(
-                out=w2_codes[:, first:first + 2, :].rearrange("p e n -> p (e n)").bitcast(FP8X4),
-                scales=w2_scales[:, first:first + 2, :].rearrange("p e n -> p (e n)"),
-                in_=w2_grouped[:, first:first + 2, :].rearrange("p e f -> p (e f)"),
+                out=w2_codes[:, first:last, :].rearrange("p e n -> p (e n)").bitcast(FP8X4),
+                scales=w2_scales[:, first:last, :].rearrange("p e n -> p (e n)"),
+                in_=w2_grouped[:, first:last, :].rearrange("p e f -> p (e f)"),
             )
 
         y_all = keep.tile([P, SLOTS], F32, name="y_all")
-        w1_codes, w1_scales, w1_grouped, acc, hidden, ys = {}, {}, {}, {}, {}, {}
+        w1_codes, w1_scales, w1_grouped, sums, ys = {}, {}, {}, {}, {}
 
-        def group_w1(e, s):
-            grouped = work.tile([P, H * PACK], BF16, name=f"w1_grouped{e}{s}", tag="w1_grouped", align_bytes=64, bufs=4)
-            dst = grouped[:].rearrange("p (t m j) -> p m t j", t=4, j=PACK)
-            src = w1_raw[e][:, s * PACK * H:(s + 1) * PACK * H].rearrange("p (j m t) -> p m t j", j=PACK, t=4)
-            cut = LAST_SCALAR_M if (e, s) == (E - 1, PASSES - 1) else SCALAR_M
-            nc.scalar.copy(out=dst[:, 0:cut], in_=src[:, 0:cut])
-            nc.vector.tensor_copy(out=dst[:, cut:P], in_=src[:, cut:P])
-            w1_grouped[e, s] = grouped
+        def copy_w1(copy, grouped, k, m, t):
+            if m.start < m.stop:
+                copy(
+                    out=grouped[:].rearrange("p (t m j) -> p m j t", t=4, j=PACK)[:, m, :, t],
+                    in_=w1_raw[k].rearrange("p (j m t) -> p m j t", j=PACK, t=4)[:, m, :, t],
+                )
 
-        def quantize_w1(e, s):
+        def group_w1(k, cut, halves):
+            grouped = work.tile([P, H * PACK], BF16, name=f"w1_grouped{k}", tag=f"slot{k % 4}", align_bytes=64, bufs=1)
+            w1_grouped[k] = grouped
+            for t in (slice(0, 2), slice(2, 4)) if halves else (slice(0, 4),):
+                copy_w1(nc.scalar.copy, grouped, k, slice(0, cut), t)
+                copy_w1(nc.vector.tensor_copy, grouped, k, slice(cut, P), t)
+
+        def quantize_w1(k, halves):
+            e, s = divmod(k, PASSES)
             if s == 0:
                 w1_codes[e] = work.tile([P, PASSES, H], U32, name=f"w1_codes{e}", tag="w1_codes", align_bytes=64)
                 w1_scales[e] = work.tile([P, PASSES, H], U8, name=f"w1_scales{e}", tag="w1_scales", align_bytes=64)
-            nc.vector.quantize_mx(
-                out=w1_codes[e][:, s, :].bitcast(FP8X4), scales=w1_scales[e][:, s, :], in_=w1_grouped[e, s][:]
-            )
+            width = H // 2 if halves else H
+            for c in range(0, H, width):
+                cols = slice(c, c + width)
+                nc.vector.quantize_mx(
+                    out=w1_codes[e][:, s, cols].bitcast(FP8X4),
+                    scales=w1_scales[e][:, s, cols],
+                    in_=w1_grouped[k][:, c * PACK:(c + width) * PACK],
+                )
 
         def pass_w1(e, s, t):
             cols, slots = slice(t * P, (t + 1) * P), slice(e * C, (e + 1) * C)
             nc.tensor.matmul_mx(
-                out=acc[e, t // 2][:, t % 2, :],
+                out=sums[e, t // 2][:, t % 2, :],
                 lhsT=w1_codes[e][:, s, cols].bitcast(FP8X4),
                 lhsT_scale=w1_scales[e][:, s, cols],
                 rhs=x_codes[:, s, slots].bitcast(FP8X4),
@@ -136,24 +160,46 @@ def tile_routed_moe_kernel(tc, xT, w1, w2, gate, offs, out):
                 stop=(s == PASSES - 1),
             )
 
-        def multiply_w1(e, s):
+        banks = {}
+
+        def multiply_w1(k):
+            e, s = divmod(k, PASSES)
             for q in range(2):
                 if s == 0:
-                    acc[e, q] = psum.tile([P, 2, C], F32, name=f"acc{e}{q}", tag=f"acc{q}")
+                    if False and e < 2:
+                        if e == 0:
+                            banks[q] = psum.tile([P, 2, 2, C], F32, name=f"acc_pair{q}")
+                        sums[e, q] = banks[q][:, e]
+                    else:
+                        sums[e, q] = psum.tile([P, 2, C], F32, name=f"acc{e}{q}", tag=f"acc{e % 2}{q}")
                 pass_w1(e, s, 2 * q)
                 if s == PASSES - 1:
                     for r in range(PASSES):
                         pass_w1(e, r, 2 * q + 1)
 
-        h_all = keep.tile([P, E, C * 4], BF16, name="h_all", align_bytes=64)
+        hidden = {}
+
+        def hidden_in(slot, pair):
+            if slot is None:
+                hidden[pair] = keep.tile([P, 2, C * 4], BF16, name=f"hidden{pair}", align_bytes=64)
+            else:
+                hidden[pair] = work.tile([P, 2, C * 4], BF16, name=f"hidden{pair}", tag=f"slot{slot % 4}", align_bytes=64, bufs=1)
 
         def apply_gelu(e):
             for q in range(2):
-                nc.scalar.activation(
-                    h_all[:, e, :].rearrange("p (n q t) -> p q n t", q=2, t=2)[:, q],
-                    acc[e, q][:].rearrange("p t n -> p n t"),
-                    GELU,
-                )
+                if False and e < 2:
+                    if e == 1:
+                        nc.scalar.activation(
+                            hidden[0][:].rearrange("p e (n q t) -> p q e n t", q=2, t=2)[:, q],
+                            banks[q][:].rearrange("p e t n -> p e n t"),
+                            GELU,
+                        )
+                else:
+                    nc.scalar.activation(
+                        hidden[e // 2][:, e % 2, :].rearrange("p (n q t) -> p q n t", q=2, t=2)[:, q],
+                        sums[e, q][:].rearrange("p t n -> p n t"),
+                        GELU,
+                    )
 
         def multiply_w2(first, last):
             count = last - first
@@ -162,9 +208,9 @@ def tile_routed_moe_kernel(tc, xT, w1, w2, gate, offs, out):
             nc.vector.quantize_mx(
                 out=h_codes[:].rearrange("p e c -> p (e c)").bitcast(FP8X4),
                 scales=h_scales[:].rearrange("p e c -> p (e c)"),
-                in_=h_all[:, first:last, :].rearrange("p e f -> p (e f)"),
+                in_=hidden[first // 2][:, first % 2:first % 2 + count, :].rearrange("p e f -> p (e f)"),
             )
-            ys[first] = psum.tile([P, count, C], F32, name=f"y{first}", tag="y")
+            ys[first] = psum.tile([P, count, C], F32, name=f"y{first}", tag=f"y{(first + 1) // 2 % 2}")
             for e in range(first, last):
                 nc.tensor.matmul_mx(
                     out=ys[first][:, e - first, :],
@@ -186,30 +232,62 @@ def tile_routed_moe_kernel(tc, xT, w1, w2, gate, offs, out):
 
         gather(0)
         group_tokens(0)
-        gather(1)
         quantize_tokens(0)
+        gather(1)
         group_tokens(1)
-        gather(2)
         quantize_tokens(1)
+        gather(2)
         group_tokens(2)
-        group_w2(0)
         quantize_tokens(2)
-        quantize_w2(0)
-        for e in range(E):
-            for s in range(PASSES):
-                group_w1(e, s)
-                quantize_w1(e, s)
-                multiply_w1(e, s)
-                if s == 0 and e > 0:
-                    apply_gelu(e - 1)
-                if s == 1 and e == 2:
-                    multiply_w2(0, 2)
-                    take_out(0, 2)
-                if s == 2 and e == 2:
-                    put_back(0, 256)
-        group_w2(2)
-        quantize_w2(2)
-        apply_gelu(E - 1)
+        group_w2(0, 2)
+        quantize_w2(0, 2)
+        group_w1(0, 48, False)
+        quantize_w1(0, False)
+        multiply_w1(0)
+        group_w1(1, 64, False)
+        quantize_w1(1, False)
+        multiply_w1(1)
+        group_w1(2, 96, False)
+        quantize_w1(2, False)
+        multiply_w1(2)
+        group_w1(3, 0, False)
+        quantize_w1(3, False)
+        multiply_w1(3)
+        group_w1(4, 64, False)
+        quantize_w1(4, False)
+        multiply_w1(4)
+        hidden_in(None, 0)
+        apply_gelu(0)
+        group_w1(5, 96, False)
+        quantize_w1(5, False)
+        multiply_w1(5)
+        group_w1(6, 0, False)
+        quantize_w1(6, False)
+        multiply_w1(6)
+        group_w1(7, 64, False)
+        quantize_w1(7, False)
+        multiply_w1(7)
+        apply_gelu(1)
+        multiply_w2(0, 2)
+        take_out(0, 2)
+        group_w1(8, 96, False)
+        quantize_w1(8, False)
+        multiply_w1(8)
+        put_back(0, 256)
+        group_w1(9, 0, False)
+        quantize_w1(9, False)
+        multiply_w1(9)
+        group_w1(10, 64, False)
+        quantize_w1(10, False)
+        multiply_w1(10)
+        hidden_in(None, 1)
+        apply_gelu(2)
+        group_w1(11, 56, False)
+        quantize_w1(11, False)
+        multiply_w1(11)
+        group_w2(2, 4)
+        quantize_w2(2, 4)
+        apply_gelu(3)
         multiply_w2(2, 4)
         take_out(2, 4)
         put_back(256, 512)

from contextlib import ExitStack

import concourse.mybir as mybir

K, T, E, C, H, N = 1536, 1536, 4, 128, 512, 128
SLOTS = E * C
P = 128
PACK = 4
K_PASS = P * PACK
PASSES = K // K_PASS
FLOPS = 2 * SLOTS * (K * H + H * N)

F32 = mybir.dt.float32
BF16 = mybir.dt.bfloat16
U32 = mybir.dt.uint32
U16 = mybir.dt.uint16
U8 = mybir.dt.uint8
FP8X4 = mybir.dt.float8_e4m3fn_x4
GELU = mybir.ActivationFunctionType.Gelu_apprx_tanh
MULT = mybir.AluOpType.mult


def tile_routed_moe_kernel(tc, xT, w1, w2, gate, offs, out):
    nc = tc.nc
    with ExitStack() as ctx:
        keep = ctx.enter_context(tc.tile_pool(name="keep", bufs=1))
        raws = ctx.enter_context(tc.tile_pool(name="raws", bufs=2))
        work = ctx.enter_context(tc.tile_pool(name="work", bufs=2))
        psum = ctx.enter_context(tc.psum_pool(name="psum", bufs=1))

        offsets = keep.tile([P, SLOTS // 16], U16, name="offsets")
        nc.sync.dma_start(offsets[:], offs)

        x_raw, w1_raw = {}, {}
        w2_raw = keep.tile([P, E, PACK * N], F32, name="w2_raw")
        gates = keep.tile([P, SLOTS], F32, name="gates")
        w1_passes = w1.rearrange("e (s p j) c -> p (e s) (j c)", p=P, j=PACK)

        def load_x(s, width):
            x_raw[s] = raws.tile([P, PACK * T], F32, name=f"x_raw{s}", tag="x_raw", bufs=3)
            rows = xT[s * K_PASS:(s + 1) * K_PASS, :].rearrange("(p j) n -> p (j n)", j=PACK)
            for j in range(0, PACK, width):
                cols = slice(j * T, (j + width) * T)
                nc.sync.dma_start(out=x_raw[s][:, cols], in_=rows[:, cols])

        def load_w2(first, last):
            nc.sync.dma_start(out=w2_raw[:, first:last, :], in_=w2[first:last].rearrange("e (p j) n -> p e (j n)", j=PACK))

        def load_gate(a, b):
            nc.sync.dma_start(out=gates[:, a:b], in_=gate[:, a:b])

        def load_w1(ks, bufs):
            raw = raws.tile([P, len(ks), PACK * H], F32, name=f"w1_raw{ks[0]}", tag=f"w1_raw{len(ks)}", bufs=bufs)
            nc.sync.dma_start(out=raw[:], in_=w1_passes[:, ks[0]:ks[-1] + 1, :])
            for i, k in enumerate(ks):
                w1_raw[k] = raw[:, i, :]

        load_x(0, 1)
        load_x(1, 1)
        load_x(2, 1)
        load_w2(0, 2)
        load_gate(0, 256)
        load_w1((0,), 8)
        load_w1((1,), 8)
        load_w1((2,), 8)
        load_w1((3,), 8)
        load_w1((4,), 8)
        load_w1((5,), 8)
        load_w1((6,), 8)
        load_w1((7,), 8)
        load_w1((8,), 8)
        load_w1((9,), 8)
        load_w1((10,), 8)
        load_w1((11,), 8)
        load_w2(2, 4)
        load_gate(256, 512)

        window = keep.tile([P, T], F32, name="window")
        nc.gpsimd.memset(window[:], 0.0)
        warm = keep.tile([P, 1], F32, name="warm")
        nc.gpsimd.memset(warm[:], 0.0)
        nc.scalar.activation(warm[:], warm[:], GELU)

        x_codes = keep.tile([P, PASSES, SLOTS], U32, name="x_codes", align_bytes=64)
        x_scales = keep.tile([P, PASSES, SLOTS], U8, name="x_scales", align_bytes=64)
        picked, x_grouped = {}, {}

        def gather(s):
            picked[s] = work.tile([P, PACK, SLOTS], F32, name=f"picked{s}", tag="picked")
            for j in range(PACK):
                nc.vector.tensor_copy(picked[s][:, j, :], x_raw[s][:, j * T:(j + 1) * T].indirect(offsets[:]))

        def group_tokens(s):
            x_grouped[s] = work.tile([P, SLOTS * PACK], BF16, name=f"x_grouped{s}", tag="x_grouped", align_bytes=64)
            nc.scalar.copy(
                out=x_grouped[s][:].rearrange("p (c i j) -> p c j i", i=4, j=PACK),
                in_=picked[s][:].rearrange("p j (c i) -> p c j i", i=4),
            )

        def quantize_tokens(s):
            nc.vector.quantize_mx(out=x_codes[:, s, :].bitcast(FP8X4), scales=x_scales[:, s, :], in_=x_grouped[s][:])

        w2_codes = keep.tile([P, E, N], U32, name="w2_codes", align_bytes=64)
        w2_scales = keep.tile([P, E, N], U8, name="w2_scales", align_bytes=64)
        w2_grouped = keep.tile([P, E, N * PACK], BF16, name="w2_grouped", align_bytes=64)

        def group_w2(first, last):
            nc.scalar.copy(
                out=w2_grouped[:, first:last, :].rearrange("p e (c i j) -> p e c j i", i=4, j=PACK),
                in_=w2_raw[:, first:last, :].rearrange("p e (j c i) -> p e c j i", i=4, j=PACK),
            )

        def quantize_w2(first, last):
            nc.vector.quantize_mx(
                out=w2_codes[:, first:last, :].rearrange("p e n -> p (e n)").bitcast(FP8X4),
                scales=w2_scales[:, first:last, :].rearrange("p e n -> p (e n)"),
                in_=w2_grouped[:, first:last, :].rearrange("p e f -> p (e f)"),
            )

        y_all = keep.tile([P, SLOTS], F32, name="y_all")
        w1_codes, w1_scales, w1_grouped, sums, ys = {}, {}, {}, {}, {}

        def copy_w1(copy, grouped, k, m, t):
            if m.start < m.stop:
                copy(
                    out=grouped[:].rearrange("p (t m j) -> p m j t", t=4, j=PACK)[:, m, :, t],
                    in_=w1_raw[k].rearrange("p (j m t) -> p m j t", j=PACK, t=4)[:, m, :, t],
                )

        def group_w1(k, cut, halves):
            grouped = work.tile([P, H * PACK], BF16, name=f"w1_grouped{k}", tag=f"slot{k % 4}", align_bytes=64, bufs=1)
            w1_grouped[k] = grouped
            for t in (slice(0, 2), slice(2, 4)) if halves else (slice(0, 4),):
                copy_w1(nc.scalar.copy, grouped, k, slice(0, cut), t)
                copy_w1(nc.vector.tensor_copy, grouped, k, slice(cut, P), t)

        def quantize_w1(k, halves):
            e, s = divmod(k, PASSES)
            if s == 0:
                w1_codes[e] = work.tile([P, PASSES, H], U32, name=f"w1_codes{e}", tag="w1_codes", align_bytes=64)
                w1_scales[e] = work.tile([P, PASSES, H], U8, name=f"w1_scales{e}", tag="w1_scales", align_bytes=64)
            width = H // 2 if halves else H
            for c in range(0, H, width):
                cols = slice(c, c + width)
                nc.vector.quantize_mx(
                    out=w1_codes[e][:, s, cols].bitcast(FP8X4),
                    scales=w1_scales[e][:, s, cols],
                    in_=w1_grouped[k][:, c * PACK:(c + width) * PACK],
                )

        def pass_w1(e, s, t):
            cols, slots = slice(t * P, (t + 1) * P), slice(e * C, (e + 1) * C)
            nc.tensor.matmul_mx(
                out=sums[e, t // 2][:, t % 2, :],
                lhsT=w1_codes[e][:, s, cols].bitcast(FP8X4),
                lhsT_scale=w1_scales[e][:, s, cols],
                rhs=x_codes[:, s, slots].bitcast(FP8X4),
                rhs_scale=x_scales[:, s, slots],
                start=(s == 0),
                stop=(s == PASSES - 1),
            )

        banks = {}

        def multiply_w1(k):
            e, s = divmod(k, PASSES)
            for q in range(2):
                if s == 0:
                    if False and e < 2:
                        if e == 0:
                            banks[q] = psum.tile([P, 2, 2, C], F32, name=f"acc_pair{q}")
                        sums[e, q] = banks[q][:, e]
                    else:
                        sums[e, q] = psum.tile([P, 2, C], F32, name=f"acc{e}{q}", tag=f"acc{e % 2}{q}")
                pass_w1(e, s, 2 * q)
                if s == PASSES - 1:
                    for r in range(PASSES):
                        pass_w1(e, r, 2 * q + 1)

        hidden = {}

        def hidden_in(slot, pair):
            if slot is None:
                hidden[pair] = keep.tile([P, 2, C * 4], BF16, name=f"hidden{pair}", align_bytes=64)
            else:
                hidden[pair] = work.tile([P, 2, C * 4], BF16, name=f"hidden{pair}", tag=f"slot{slot % 4}", align_bytes=64, bufs=1)

        def apply_gelu(e):
            for q in range(2):
                if False and e < 2:
                    if e == 1:
                        nc.scalar.activation(
                            hidden[0][:].rearrange("p e (n q t) -> p q e n t", q=2, t=2)[:, q],
                            banks[q][:].rearrange("p e t n -> p e n t"),
                            GELU,
                        )
                else:
                    nc.scalar.activation(
                        hidden[e // 2][:, e % 2, :].rearrange("p (n q t) -> p q n t", q=2, t=2)[:, q],
                        sums[e, q][:].rearrange("p t n -> p n t"),
                        GELU,
                    )

        def multiply_w2(first, last):
            count = last - first
            h_codes = keep.tile([P, count, C], U32, name=f"h_codes{first}", align_bytes=64)
            h_scales = keep.tile([P, count, C], U8, name=f"h_scales{first}", align_bytes=64)
            nc.vector.quantize_mx(
                out=h_codes[:].rearrange("p e c -> p (e c)").bitcast(FP8X4),
                scales=h_scales[:].rearrange("p e c -> p (e c)"),
                in_=hidden[first // 2][:, first % 2:first % 2 + count, :].rearrange("p e f -> p (e f)"),
            )
            ys[first] = psum.tile([P, count, C], F32, name=f"y{first}", tag=f"y{(first + 1) // 2 % 2}")
            for e in range(first, last):
                nc.tensor.matmul_mx(
                    out=ys[first][:, e - first, :],
                    lhsT=w2_codes[:, e, :].bitcast(FP8X4),
                    lhsT_scale=w2_scales[:, e, :],
                    rhs=h_codes[:, e - first, :].bitcast(FP8X4),
                    rhs_scale=h_scales[:, e - first, :],
                    start=True,
                    stop=True,
                )

        def take_out(first, last):
            nc.scalar.copy(y_all[:, first * C:last * C], ys[first][:].rearrange("p e c -> p (e c)"))

        def put_back(a, b):
            nc.vector.tensor_tensor(
                window[:].indirect(offsets[:, a // 16:b // 16]), y_all[:, a:b], gates[:, a:b], MULT
            )

        gather(0)
        group_tokens(0)
        quantize_tokens(0)
        gather(1)
        group_tokens(1)
        quantize_tokens(1)
        gather(2)
        group_tokens(2)
        quantize_tokens(2)
        group_w2(0, 2)
        quantize_w2(0, 2)
        group_w1(0, 48, False)
        quantize_w1(0, False)
        multiply_w1(0)
        group_w1(1, 64, False)
        quantize_w1(1, False)
        multiply_w1(1)
        group_w1(2, 96, False)
        quantize_w1(2, False)
        multiply_w1(2)
        group_w1(3, 0, False)
        quantize_w1(3, False)
        multiply_w1(3)
        group_w1(4, 64, False)
        quantize_w1(4, False)
        multiply_w1(4)
        hidden_in(None, 0)
        apply_gelu(0)
        group_w1(5, 96, False)
        quantize_w1(5, False)
        multiply_w1(5)
        group_w1(6, 0, False)
        quantize_w1(6, False)
        multiply_w1(6)
        group_w1(7, 64, False)
        quantize_w1(7, False)
        multiply_w1(7)
        apply_gelu(1)
        multiply_w2(0, 2)
        take_out(0, 2)
        group_w1(8, 96, False)
        quantize_w1(8, False)
        multiply_w1(8)
        put_back(0, 256)
        group_w1(9, 0, False)
        quantize_w1(9, False)
        multiply_w1(9)
        group_w1(10, 64, False)
        quantize_w1(10, False)
        multiply_w1(10)
        hidden_in(None, 1)
        apply_gelu(2)
        group_w1(11, 56, False)
        quantize_w1(11, False)
        multiply_w1(11)
        group_w2(2, 4)
        quantize_w2(2, 4)
        apply_gelu(3)
        multiply_w2(2, 4)
        take_out(2, 4)
        put_back(256, 512)
        nc.sync.dma_start(out=out, in_=window[:])
